import numpy as np, ml_dtypes
CORES = [10,34,74,98]
N = 4
import mx_ref
BF = ml_dtypes.bfloat16
def gentries(a):
    return np.ascontiguousarray(a.reshape(8, 16, -1).transpose(0, 2, 1)).reshape(8, -1)
def gtable(e):
    e = np.asarray(e); return np.ascontiguousarray(e.reshape(8, -1, 16).transpose(0, 2, 1)).reshape(128, -1).astype(np.int32)
def gcols(t, e):
    v = np.concatenate([t.reshape(8, 16, -1, 4), np.zeros((8, 16, 1, 4), BF)], axis=2)
    return np.ascontiguousarray(np.stack([v[g][:, e[g]] for g in range(8)])).reshape(128, -1)
def tile(rs):
    return np.stack(rs, axis=2).reshape(128, -1).astype(BF)
def pick(q, e):
    c = np.concatenate([q[0].reshape(128, -1, 4), np.zeros((128, 1, 4), np.uint8)], axis=1); s = np.concatenate([q[1], np.ones((16, 1), np.uint8)], axis=1)
    return (np.ascontiguousarray(c[:, e].reshape(128, -1)), np.ascontiguousarray(s[:, e]))
def join(*qs):
    return (np.concatenate([q[0] for q in qs], axis=1), np.concatenate([q[1] for q in qs], axis=1))
def put(q, e, v):
    c, s = q[0].reshape(128, -1, 4).copy(), q[1].copy(); c[:, e] = v[0].reshape(128, -1, 4); s[:, e] = v[1]
    return (c.reshape(128, -1), s)
def pk(c, s):
    return (np.ascontiguousarray(c), mx_ref.live(s))
def emit(q):
    return q[0], q[1]
def packed(v, rng):
    q = [mx_ref.quantize(np.ascontiguousarray(v[r])) for r in range(N)]
    return np.stack([a for a, b in q]), np.stack([mx_ref.plane(b, rng) for a, b in q])
def values_of_codes():
    e, c = np.zeros((128, 128, 4), np.float32), np.zeros((128, 2, 4), np.uint8)
    e[np.arange(128), np.arange(128), 0] = 1
    c[:127, :, 0] = np.arange(256).reshape(2, 128).T[:127]
    return mx_ref.matmul(mx_ref.quantize(e.reshape(128, 512).astype(BF)), (c.reshape(128, 8), np.full((16, 2), 127, np.uint8))).T.reshape(-1).astype(np.float64)
CODE_VALUE, SCALE_VALUE = values_of_codes(), 2.0 ** (np.arange(256) - 127.0)
def decode(q):
    return (CODE_VALUE[q[0]].reshape(16, 8, -1, 4) * SCALE_VALUE[q[1]][:, None, :, None] + 0.0).reshape(128, -1).astype(np.float32)
def f(rng, *shape):
    return mx_ref.flush((rng.standard_normal(shape, dtype=np.float32) * np.exp2(rng.integers(-2, 3, shape[:-1] + (1,)))).astype(BF))
def wide(rng, *shape, cols=0):
    v = rng.standard_normal(shape, dtype=np.float32) * np.exp2(rng.integers(-12, 13, shape)).astype(np.float32)
    if cols: v *= np.repeat(np.exp2(rng.integers(-cols, cols + 1, shape[:-2] + (1, shape[-1] // 4))) * (rng.random(shape[:-2] + (1, shape[-1] // 4)) > 0.0625), 4, axis=-1).astype(np.float32)
    return mx_ref.flush(v.astype(BF))
C, HALF = 384, 192
MASK = [1, 2, 3]
def numbers_of(rng):
    return {"x": np.array(f(rng, N, 128, 4 * C)), "u": np.array(f(rng, N, 128, 512)), "v": np.array(f(rng, N, 128, 512))}
def orders(rng):
    e = np.tile(np.arange(C), (N, 8, 1))
    k = [rng.permuted(e, axis=2) for i in range(4)]
    t = np.zeros((N, 8, C), np.int64)
    np.put_along_axis(t, k[3], np.ascontiguousarray(k[3].reshape(N, 8, HALF, 2)[:, :, :, ::-1]).reshape(N, 8, C), axis=2)
    return k[:3] + [t]
def stored(k):
    return {n: np.stack([gtable(a[r]) for r in range(N)]) for n, a in zip(("lg", "pb", "fd", "ex"), k)}
def lists(rng):
    return stored(orders(rng))
def layers(rng):
    return np.array(f(rng, N, 128, 2048)).reshape(N, 8, 16, 4, 8, 16, 4)
def weights(rng, w):
    c, p = packed(np.ascontiguousarray(w).reshape(N, 128, 2048), rng)
    return {"wc": c, "ws": p}
def setup_inputs(rng):
    return {**numbers_of(rng), **lists(rng), **weights(rng, layers(rng))}
def setup_inputs_ties(rng):
    d = numbers_of(rng)
    o = rng.permutation(N)
    k = rng.integers(-1, 2, (N, 8, 4, C)).astype(np.float32)
    k[o[1]] = 1
    k[o[2]] = -1
    x = d["x"].reshape(N, 8, 16, C, 4)
    x[:, :, :4] = 0
    x[:, :, :4, :, 0] = k.astype(BF)
    u = d["u"].reshape(N, 8, 16, 8, 16, 4)
    u[:, :, :, :, :4] = 0
    for g in range(8):
        for j in range(4): u[:, g, j, g, j, 0] = 1.0
    u[o[0], :, :, :, :4] = 0
    w = layers(rng)
    w[:, :, :, :, :, :4] = 0
    return {"x": x.reshape(N, 128, 4 * C), "u": u.reshape(N, 128, 512), "v": d["v"], **lists(rng), **weights(rng, w)}
def setup_inputs_near(rng):
    d = numbers_of(rng)
    o = rng.permutation(N)
    k = np.ones(N, np.float32)
    k[o[:N // 2]] = 2.0 ** -30
    s = rng.integers(-1, 2, (N, 8, 4, C)) * np.where(k < 1, 2 * k, k)[:, None, None, None]
    x = d["x"].astype(np.float32).reshape(N, 8, 16, C, 4)
    x[:, :, :8] = 0
    x[:, :, 0:8:2, :, 0] = 1.125 * s
    x[:, :, 1:8:2, :, 0] = -1.25 * s
    for r in range(N):
        at_ = [0, C - 1, int(rng.integers(C)), int(rng.integers(C))]
        for g, c in zip(rng.permutation(8)[:4], at_): x[r, g, 2 * rng.integers(4), c, 0] = 2.0 ** 30 * rng.choice([-1.0, 1.0])
    x[o[0], :, 8:] = 0
    x[o[0], :, 12:, :, 0] = rng.choice([-1.0, 1.0], (8, 4, C)) * 2.0 ** -30
    x[o[0], :, 12, :, 2] = 2.0 ** -30
    u = d["u"].reshape(N, 8, 16, 8, 16, 4)
    u[:, :, :, :, :4] = 0
    w = np.zeros((N, 8, 16, 4, 8, 16, 4), np.float32)
    for g in range(8):
        for j in range(4):
            u[:, g, 2 * j, g, j, 0] = (1.125 * k).astype(np.float32).astype(BF)
            u[:, g, 2 * j + 1, g, j, 0] = k.astype(BF)
            w[:, g, 12 + j, 0, g, 8 + j, 0] = 1.125 * 2.0 ** -8
            w[:, g, 12 + j, 1, g, 8 + (j + 1) % 4, 0] = -1.25 * 2.0 ** -8
        w[:, g, 12, 1, g, 12, 2] = 2.0 ** 5
    u[o[0], :, :, :, :4] = 0
    for g in range(8):
        for j in range(4):
            u[o[0], g, 8 + j, g, j, 0] = 1.125 * 2.0 ** -30
            u[o[0], g, 8 + (j + 1) % 4, g, j, 1] = 2.0 ** -30
    return {"x": x.reshape(N, 128, 4 * C).astype(BF), "u": u.reshape(N, 128, 512), "v": d["v"], **lists(rng), **weights(rng, w.astype(BF))}
def setup_inputs_odd(rng):
    d = numbers_of(rng)
    x = np.zeros((N, 8, 16, C, 4), np.float32)
    x[:, :, 0, :, 1] = 1.96875 * 2.0 ** 8 * rng.choice([-1.0, 1.0], (N, 8, C))
    x[:, :, :4, :, 0] = -(8 + rng.integers(0, 2, (N, 8, 4, C))) * 2.0 ** -8
    x[:, :, 4:8, :, 0] = 8 * 2.0 ** -8
    a = np.exp2(rng.integers(-3, 4, 8).astype(np.float32))[None, :, None]
    x[:, :, 8, :, 0] = -2.953125 * a
    x[:, :, 12, :, 0] = -1.125 * a
    x[:, :, 14, :, 0] = -0.0703125 * a
    u = d["u"].reshape(N, 8, 16, 8, 16, 4)
    u[:, :, :, :, :4] = 0
    w = np.zeros((N, 8, 16, 4, 8, 16, 4), np.float32)
    for g in range(8):
        for j in range(4):
            u[:, g, j, g, j, 0] = 1.0
            u[:, g, 4 + j, g, j, 0] = 1.0
            w[:, g, 14, j, g, 9, 0] = -2.0 ** (j - 5)
        w[:, g, 12, 0, g, 8, 0] = -28.0
    return {"x": x.reshape(N, 128, 4 * C).astype(BF), "u": u.reshape(N, 128, 512), "v": d["v"], **lists(rng), **weights(rng, w.astype(BF))}
def setup_inputs_ends(rng):
    d = numbers_of(rng)
    o, e = rng.permutation(N) % 4, rng.permutation(N) % 4
    s = rng.choice([-1.0, 1.0], (N, 128, C, 4))
    s[o == 0] = -1
    s[o == 1] = rng.choice([-1.0, 1.0], (N, 1, C, 1))[o == 1]
    for r in range(N):
        if o[r] == 3: s[r, ::8, :, 0] = 1
    x = s * (0.955 + 0.02 * rng.random((N, 128, C, 4))) * 2.0 ** 30
    x[o == 3] = s[o == 3] * 2.0 ** -30
    size = np.where(o == 3, 2.0 ** -30, 2.0 ** 30)
    a = np.stack([rng.permutation(32).reshape(8, 4) % 2 * 2.0 - 1.0 for r in range(N)]) * size[:, None, None]
    u = d["u"].reshape(N, 128, 8, 16, 4)
    u[:, :, :, :4] = a.astype(np.float32).astype(BF)[:, None, :, :, None]
    v = rng.choice([-1.0, 1.0], (N, 128, 512)) * size[:, None, None]
    c = np.arange(C)
    plain, pairs = [c, c[::-1], (c + 1) % C], [c[::-1], c ^ 1, (c + HALF) % C]
    k = orders(rng)
    for r in range(N):
        if e[r] < 3:
            for n in range(3): k[n][r] = plain[(e[r] + n) % 3]
            k[3][r] = pairs[e[r]]
    h = np.where(o == 3, 32.0, -0.125)[:, None] * np.ones((1, 128))
    for r in range(N):
        if o[r] == 3:
            h[r, 14::16] = 2.0 ** -8
            h[r, 15::16] = 2.0 ** 8
        else: h[r, 15::16] = 0
    w = np.zeros((N, 128, 4, 128, 4), np.float32)
    i = np.arange(128)
    for b in range(4): w[:, i, b, i, b] = h
    return {"x": x.astype(np.float32).reshape(N, 128, 4 * C).astype(BF), "u": u.reshape(N, 128, 512), "v": v.astype(np.float32).astype(BF), **stored(k), **weights(rng, w.astype(BF))}
def setup_inputs_spread(rng):
    d = setup_inputs(rng)
    d["x"] = wide(rng, N, 128, 4 * C, cols=6)
    return d
def check_inputs(d):
    b = []
    for k in ("x", "u", "v"):
        a = np.abs(d[k].astype(np.float32))
        if not (np.isfinite(a).all() and ((a == 0) | (a >= 2.0 ** -30) & (a <= 2.0 ** 30)).all()): b.append("a value of " + k)
    for k in ("lg", "pb", "fd"):
        if not (np.sort(d[k].reshape(N, 8, C), axis=2) == np.arange(C)).all(): b.append(k + ": no permutation")
    for r in range(N):
        e = gentries(d["ex"][r])
        if not ((e >= 0) & (e < C)).all(): b.append("an entry of ex")
        elif (e == np.arange(C)).any() or (at(e, e) != np.arange(C)).any(): b.append("ex: no pairs")
    none, least, most = [emit(mx_ref.quantize(np.full((128, 16), k, np.float32).astype(BF)))[1][0, 0] for k in (0.0, 2.0 ** -8, 2.0 ** 8)]
    for r in range(N):
        if ((d["wc"][r] == 0x7F) | (d["wc"][r] == 0xFF)).any(): b.append("wc: a code that is no number")
        s = mx_ref.live(d["ws"][r])
        if ((s != none) & ((s < least) | (s > most))).any(): b.append("ws: a scale out of range")
        if (((d["wc"][r].reshape(16, 8, 512, 4) & 0x7F) != 0) & (s == none)[:, None, :, None]).any(): b.append("wc: a code other than zero under the scale of zeros")
    return b
def at(t, e):
    return np.take_along_axis(t, e.astype(np.int64), axis=1)
def reference(x, u, v, lg, pb, fd, ex, wc, ws):
    qu = [mx_ref.quantize(u[r]) for r in range(N)]
    lay = [pk(wc[r], ws[r]) for r in range(N)]
    leg, back, fore, pair = [[gentries(t[r]) for r in range(N)] for t in (lg, pb, fd, ex)]
    now = [x[r] for r in range(N)]
    for mask in MASK:
        made, swapped = [], []
        for r in range(N):
            s = mx_ref.matmul(qu[r], mx_ref.quantize(now[r])).reshape(8, 16, C)
            low = np.minimum(np.arange(C), pair[r])
            turn = [np.where(at(s[:, j], low) < 0, pair[r], np.arange(C)) for j in range(4)]
            for j, b in enumerate((back[r ^ mask], back[r], back[r ^ mask])):
                leg[r] = at(b, at(turn[j], at(leg[r], fore[r])))
            swapped.append(at(back[r], turn[3]))
            z = (gcols(now[r], leg[r]).astype(np.float32) + gcols(now[r], at(leg[r], fore[r])).astype(np.float32)) * np.float32(0.5)
            q = mx_ref.quantize(z.astype(BF))
            made.append(tile([mx_ref.matmul(pick(lay[r], np.arange(128 * b, 128 * b + 128)), q) * np.float32(0.03125) for b in range(4)]))
        new = []
        for r in range(N):
            m = at(fore[r], leg[r])
            far = gcols(decode(mx_ref.quantize(made[r ^ mask])).astype(BF), m[:, :HALF])
            near = gcols(made[r], m[:, HALF:])
            new.append((now[r].astype(np.float32) + np.concatenate([far, near], axis=1).astype(np.float32)).astype(BF))
        now, back = new, swapped
    y, pl = np.zeros((N, 128, C), np.float32), np.zeros((N, 8, 2 * C), np.float32)
    oc, osc = np.zeros((N, 128, 4 * C), np.uint8), np.zeros((N, 16, C), np.uint8)
    for r in range(N):
        q = mx_ref.quantize(now[r])
        y[r] = mx_ref.matmul(mx_ref.quantize(v[r]), q)
        pl[r] = np.concatenate([leg[r], back[r]], axis=1)
        oc[r], osc[r] = emit(q)
    return {"y": y, "pl": pl, "oc": oc, "osc": osc}

@@ -1,0 +1,465 @@
+from concourse.mybir import dt, AluOpType, ActivationFunctionType
+
+MASKS = [1, 2, 3]
+FRAC = 4096.0
+CUT = 256
+
+_BF, _F32, _I32, _U16, _X4, _U8 = "bfloat16", "float32", "int32", "uint16", "float8_e4m3fn_x4", "uint8"
+_SB = {
+    "X": (1536, _BF), "ub": (512, _BF), "vb": (512, _BF),
+    "lgi": (24, _I32), "pbi": (24, _I32), "fdi": (24, _I32), "exi": (24, _I32),
+    "wq": (512, _X4), "wp": (512, _U8), "uq": (128, _X4), "up": (128, _U8), "vq": (128, _X4), "vp": (128, _U8),
+    "ones": (512, _BF), "et": (2048, _BF), "eq": (512, _X4), "ep": (512, _U8),
+    "idw": (384, _F32), "ids": (384, _F32), "mask": (384, _F32), "reset": (384, _BF), "FP": (384, _F32), "cq": (384, _F32),
+    "pi": (2, _I32), "ti": (16, _I32), "tf": (2, _F32), "lsi": (8, _F32), "LS": (8, _U16),
+    "i16": (24, _F32), "pqi": (2, _I32), "pqf": (2, _F32), "idc": (24, _F32), "Emin": (24, _F32),
+    "Fc": (24, _U16), "Yc": (24, _U16), "Ec": (24, _U16), "mE": (26, _U16), "Pc": (24, _U16), "Qc": (24, _U16),
+    "base": (128, _F32), "dif": (128, _F32), "FD": (128, _F32), "M": (128, _F32), "Mc": (96, _U16), "Rc": (24, _U16),
+    "W0": (384, _F32), "W1": (384, _F32), "W2": (384, _F32), "Pw": (384, _F32), "Qw": (384, _F32), "Yw": (384, _F32),
+    "G1": (384, _F32), "G2": (384, _F32),
+    "DM": (384, _F32), "SC": (384, _F32), "DM2": (384, _F32), "SC2": (384, _F32), "DM3": (384, _F32), "SC3": (384, _F32),
+    "l4": (96, _U16), "ki": (24, _I32), "kc": (12, _U16), "kp": (12, _U16), "t1": (32, _F32),
+    "V": (1536, _BF), "V2": (1536, _BF), "z": (1536, _BF), "H": (1536, _BF), "hs": (768, _BF),
+    "zq": (384, _X4), "zp": (384, _U8), "qx": (384, _X4), "qp": (384, _U8),
+    "rb": (384, _BF), "G": (400, _BF), "TR": (768, _BF),
+    "ys": (384, _F32), "yo": (384, _F32), "po": (384, _F32),
+    "pn1": (24, _F32), "pn2": (24, _F32), "pland1": (24, _I32), "pland2": (24, _F32), "pland3": (24, _F32),
+}
+for _n in (1, 2, 3):
+    _SB["kk%d" % _n] = (24, _I32)
+    _SB["kland%d" % _n] = (12, _I32)
+    _SB["hq%d" % _n] = (192, _X4)
+    _SB["hp%d" % _n] = (192, _U8)
+    _SB["hlq%d" % _n] = (192, _X4)
+    _SB["hlp%d" % _n] = (192, _U8)
+SCRATCH = {k: ("sbuf", [128, n], d) for k, (n, d) in _SB.items()}
+SCRATCH["psA"] = ("psum", [128, 2048], "float32")
+SCRATCH["psB"] = ("psum", [128, 2048], "float32")
+SEMAPHORES = (["qg", "qv", "qa", "qt", "snd", "stS", "stA"]
+              + ["ld_" + k for k in ("x0", "x1", "u", "v", "lg", "pb", "fd", "ex", "wc", "ws")]
+              + ["%s%d" % (k, n) for k in ("aP", "aK", "aH") for n in (1, 2, 3)])
+
+
+def r(name, lo=0, hi=None, step=1):
+    return (name, lo, _SB[name][0] if hi is None else hi, step)
+
+
+def ps(name, bank, n):
+    return (name, 512 * bank, 512 * bank + n, 1)
+
+
+def region(v):
+    if v[0] in ("psA", "psB"):
+        return (v[0], v[1] - v[1] % 512, v[1] - v[1] % 512 + 512, 1)
+    return v
+
+
+def meet(a, b):
+    if a[1] >= b[2] or b[1] >= a[2]:
+        return False
+    return not (a[3] > 1 and a[3] == b[3] and a[1] % a[3] != b[1] % b[3])
+
+
+def covers(a, b):
+    return a[1] <= b[1] and b[2] <= a[2] and (a[3] == 1 or (a[3] == b[3] and a[1] % a[3] == b[1] % b[3]))
+
+
+def machine(g, T):
+    eng = {"g": g, "v": g.vector, "a": g.scalar, "t": g.tensor, "s": g.sync}
+    count, seen, snap, log = {q: 0 for q in eng}, {q: {} for q in eng}, {}, {}
+
+    def need(q, toks):
+        want = {}
+        for s, n in toks:
+            if seen[q].get(s, 0) < n:
+                want[s] = max(n, want.get(s, 0))
+        for s in sorted(want):
+            n = want[s]
+            if any(o != s and snap.get((o, m), {}).get(s, 0) >= n for o, m in want.items()):
+                continue
+            eng[q].wait_ge(T.sem[s], n)
+            seen[q][s] = max(n, seen[q].get(s, 0))
+            for k, m in snap.get((s, n), {}).items():
+                seen[q][k] = max(m, seen[q].get(k, 0))
+
+    def deps(q, reads, writes):
+        toks = []
+        for v in [region(x) for x in reads]:
+            bank = v[0] in ("psA", "psB")
+            for w, kind, oq, tok in log.get(v[0], []):
+                if meet(v, w) and (kind == "w" or (bank and oq != q)):
+                    toks.append(tok)
+        for v in [region(x) for x in writes]:
+            for w, kind, oq, tok in log.get(v[0], []):
+                if meet(v, w) and (kind == "w" or oq != q):
+                    toks.append(tok)
+        return toks
+
+    def note(q, reads, writes, tok):
+        for v in [region(x) for x in writes]:
+            log[v[0]] = [e for e in log.get(v[0], []) if not covers(v, e[0])] + [(v, "w", q, tok)]
+        for v in [region(x) for x in reads]:
+            log.setdefault(v[0], []).append((v, "r", q, tok))
+
+    def op(q, call, reads, writes):
+        need(q, deps(q, reads, writes))
+        count[q] += 1
+        tok = ("q" + q, count[q])
+        snap[tok] = dict(seen[q])
+        call(eng[q]).then_inc(T.sem[tok[0]], 1)
+        note(q, reads, writes, tok)
+
+    def arrived(tok, writes):
+        note("", [], writes, tok)
+
+    return eng, op, need, deps, arrived, count
+
+
+def rank_program(g, core, T, topo):
+    rank = T.rank_of(core)
+    if rank is None:
+        return
+    A, F = AluOpType, ActivationFunctionType
+    eng, op, need, deps, arrived, count = machine(g, T)
+    sent, stores = [0], {"s": 0, "a": 0}
+
+    def ap(v):
+        t = T[v[0]]
+        return t[:, v[1]:v[2]] if v[3] == 1 else t[:, v[1]:v[2]:v[3]]
+
+    def ind(w, o):
+        return ap(w).indirect(ap(o))
+
+    def copy(o, i):
+        op("v", lambda e: e.tensor_copy(ap(o), ap(i)), [i], [o])
+
+    def ts(o, i, s1, s2, *ops):
+        op("v", lambda e: e.tensor_scalar(ap(o), ap(i), s1, s2, *ops), [i], [o])
+
+    def tsp(o, i, col, s2, *ops):
+        op("v", lambda e: e.tensor_scalar(ap(o), ap(i), ap(col), s2, *ops), [i, col], [o])
+
+    def tt(o, i, j, f):
+        op("v", lambda e: e.tensor_tensor(ap(o), ap(i), ap(j), f), [i, j], [o])
+
+    def gtt(o, w, l, j, f):
+        op("v", lambda e: e.tensor_tensor(ap(o), ind(w, l), ap(j), f), [w, l, j], [o])
+
+    def gts(o, w, l, s1, f):
+        op("v", lambda e: e.tensor_scalar(ap(o), ind(w, l), s1, None, f), [w, l], [o])
+
+    def gcopy(o, w, l):
+        op("v", lambda e: e.tensor_copy(ap(o), ind(w, l)), [w, l], [o])
+
+    def quant(c, s, t):
+        op("v", lambda e: e.quantize_mx(ap(c), ap(s), ap(t)), [t], [c, s])
+
+    def turn(o, i):
+        op("v", lambda e: e.transpose(ap(o), ap(i)), [i], [o])
+
+    def scan(o, i):
+        op("v", lambda e: e.tensor_tensor_scan(ap(o), ap(r("reset")), ap(i), 0.0, A.mult, A.add), [r("reset"), i], [o])
+
+    def act(o, i, f=None, scale=1.0):
+        op("a", lambda e: e.activation(ap(o), ap(i), F.Copy if f is None else f, scale=scale), [i], [o])
+
+    def gact(o, w, l, f=None, scale=1.0):
+        op("a", lambda e: e.activation(ap(o), ind(w, l), F.Copy if f is None else f, scale=scale), [w, l], [o])
+
+    def mm(o, lc, ls, rc, rs):
+        op("t", lambda e: e.matmul_mx(ap(o), ap(lc), ap(ls), ap(rc), ap(rs), True, True), [lc, ls, rc, rs], [o])
+
+    def gboth(o, w, l):
+        gcopy(r(o, 0, 192), r(w), (l[0], l[1], l[1] + 12, 1))
+        gact(r(o, 192, 384), r(w), (l[0], l[1] + 12, l[1] + 24, 1))
+
+    def iota(o, pattern, base, cm):
+        if _SB[o[0]][1] == _F32:
+            op("g", lambda e: e.iota(ap(o), pattern, base, cm, allow_small_or_imprecise_dtypes=True), [], [o])
+        else:
+            op("g", lambda e: e.iota(ap(o), pattern, base, cm), [], [o])
+
+    def keep(o, i, pattern, f, base, cm):
+        op("g", lambda e: e.affine_select(ap(o), ap(i), pattern, f, 0.0, base, cm), [i], [o])
+
+    def load(q, sem, o, src, v):
+        eng[q].dma_start(o, src).then_inc(T.sem["ld_" + sem], 16)
+        arrived(("ld_" + sem, 16), [v])
+
+    def store(q, o, i, v):
+        need(q, deps(q, [v], []))
+        eng[q].dma_start(o, i).then_inc(T.sem["stS" if q == "s" else "stA"], 16)
+        stores[q] += 16
+
+    def send(to, o, i, v, sem):
+        need("g", deps("g", [v], []))
+        dst = T.cores[to]
+        rid, pid = topo.addr(dst)[:2]
+        g.remote_dma(o, i, T.sem[sem], T.sem.snd, pid, rid, topo.mask(core, dst))
+        sent[0] += len(topo.engines(core, dst))
+
+    def landed(frm, sem, views, calls=1):
+        arrived((sem, calls * len(topo.engines(T.cores[frm], core))), views)
+
+    def last(n):
+        return r(n, 15, 384, 16)
+
+    def slot(n, k):
+        return r(n, 32 * k, 32 * k + 24)
+
+    load("s", "pb", ap(r("pbi")), T.pb[:, :], r("pbi"))
+    load("s", "ex", ap(r("exi")), T.ex[:, :], r("exi"))
+    load("a", "fd", ap(r("fdi")), T.fd[:, :], r("fdi"))
+    load("a", "lg", ap(r("lgi")), T.lg[:, :], r("lgi"))
+    load("s", "x0", ap(r("X", 0, 768)), T.x[:, 0:768], r("X", 0, 768))
+    load("a", "u", ap(r("ub")), T.u[:, :], r("ub"))
+    load("s", "x1", ap(r("X", 768, 1536)), T.x[:, 768:1536], r("X", 768, 1536))
+    load("s", "wc", T.wq[:, :].bitcast(dt.uint8), T.wc[:, :], r("wq"))
+    load("s", "ws", ap(r("wp")), T.ws[:, :], r("wp"))
+    load("s", "v", ap(r("vb")), T.v[:, :], r("vb"))
+    p1 = rank ^ MASKS[0]
+    landed(p1, "aP1", [r("pland1")])
+
+    iota(r("pi"), [[0, 2]], 0, 1)
+    iota(r("lsi", 0, 6), [[-1, 3], [256, 2]], 2, 0)
+    iota(r("lsi", 6, 8), [[256, 2]], 3, 0)
+    iota(r("i16"), [[16, 24]], 0, 0)
+    iota(r("idw"), [[1, 384]], 0, 0)
+    iota(r("cq"), [[0, 24], [1, 16]], 0, 0)
+    send(p1, ap(r("pland1")), ap(r("pbi")), r("pbi"), "aP1")
+    op("v", lambda e: e.memset(ap(r("ones")), 1.0), [], [r("ones")])
+    op("v", lambda e: e.memset(ap(r("base")), 0.0), [], [r("base")])
+    op("v", lambda e: e.memset(ap(r("dif")), 0.0), [], [r("dif")])
+    keep(r("reset"), r("ones", 0, 384), [[0, 24], [1, 16]], A.is_ge, -1, 0)
+    for b in range(4):
+        keep(r("et", 512 * b, 512 * b + 512), r("ones"), [[-1, 512]], A.is_equal, b, 4)
+
+    def t1(k):
+        return r("ti", k, k + 1)
+    pi, pqi, pqf = r("pi", 0, 1), r("pqi", 0, 1), r("pqf", 0, 1)
+    ts(pqi, pi, 15, None, A.bitwise_and)
+    ts(t1(0), pi, 4, 1, A.logical_shift_right, A.bitwise_and)
+    copy(pqf, pqi)
+    tt(t1(1), pi, t1(0), A.add)
+    ts(t1(2), pqi, 0, 384, A.is_equal, A.mult)
+    ts(t1(3), pqi, 16, None, A.mult)
+    ts(t1(4), t1(1), 1, None, A.bitwise_and)
+    tt(t1(5), t1(2), t1(0), A.mult)
+    tsp(r("idc"), r("i16"), pqf, None, A.add)
+    ts(t1(6), t1(4), 368, None, A.mult)
+    tt(r("tf", 0, 1), t1(6), t1(3), A.add)
+    tt(r("tf", 1, 2), r("tf", 0, 1), t1(5), A.add)
+    tsp(r("LS", 1, 8, 2), r("lsi", 1, 8, 2), r("tf", 0, 1), 767.0, A.add, A.min)
+    tsp(r("LS", 0, 8, 2), r("lsi", 0, 8, 2), r("tf", 1, 2), 767.0, A.add, A.min)
+    act(r("ids"), r("idw"), scale=1.0 / FRAC)
+    act(slot("base", 0), r("idc"))
+    act(slot("base", 2), r("idc"))
+
+    copy(r("Pc"), r("pbi"))
+    copy(r("Yc"), r("lgi"))
+    gact(r("Pw"), r("idw"), r("Pc"))
+    gact(r("Yw"), r("idw"), r("Yc"))
+    copy(r("Fc"), r("fdi"))
+    tt(r("Emin"), r("exi"), r("idc"), A.min)
+    copy(r("Ec"), r("exi"))
+    tt(slot("dif", 0), r("exi"), r("idc"), A.subtract)
+    copy(r("mE", 0, 24), r("Emin"))
+    copy(r("mE", 24, 25), r("Emin", 0, 1))
+    copy(slot("base", 1), r("pbi"))
+    gtt(r("FP"), r("ids"), r("Fc"), r("idw"), A.add)
+    gact(r("G1"), r("Yw"), r("Fc"))
+    tsp(r("mask"), r("cq"), pqf, None, A.is_equal)
+    quant(r("uq"), r("up"), r("ub"))
+
+    def qx(half):
+        c = r("qx", 192 * half, 192 * half + 192)
+        s = r("qp", 192 * half, 192 * half + 192)
+        quant(c, s, r("X", 768 * half, 768 * half + 768))
+        return c, s
+
+    def scores(half, cs):
+        mm(ps("psB", half, 192), r("uq"), r("up"), cs[0], cs[1])
+
+    def signs(half, q):
+        o = ps("psB", half, 192)
+        d = r("rb", 192 * half, 192 * half + 192)
+        if q == "v":
+            ts(d, o, -1.0, 0.0, A.mult, A.max)
+        else:
+            act(d, o, F.Relu, -1.0)
+
+    gact(r("G2"), r("G1"), r("Fc"))
+    scores(0, qx(0))
+    gtt(r("DM2"), r("Pw"), r("Ec"), r("mask"), A.mult)
+    scores(1, qx(1))
+    signs(0, "a")
+    signs(1, "a")
+    scan(r("SC2"), r("DM2"))
+    act(slot("dif", 2), slot("dif", 0))
+    tt(slot("dif", 1), last("SC2"), slot("base", 1), A.subtract)
+    act(slot("base", 3), slot("base", 1))
+    act(slot("dif", 3), slot("dif", 1))
+
+    def next_legs():
+        gtt(r("DM3"), r("G2"), r("Fc"), r("mask"), A.mult)
+        scan(r("SC3"), r("DM3"))
+        copy(r("Rc"), last("SC3"))
+
+    for n in (1, 2, 3):
+        me = str(n)
+        mate = rank ^ MASKS[n - 1]
+        landed(mate, "aK" + me, [r("kland" + me)])
+        landed(mate, "aH" + me, [r("hlq" + me), r("hlp" + me)], 2)
+        if n > 1:
+            scores(0, qx(0))
+            signs(0, "v")
+        gts(r("G", 0, 192), r("rb"), r("mE", 0, 12), 0.0, A.is_gt)
+        gact(r("G", 192, 400), r("rb"), r("mE", 12, 25), F.Sign)
+        turn(r("TR", 0, 384), r("G", 0, 384))
+        turn(r("TR", 384, 768), r("G", 16, 400))
+        runs = [(0, 32), (32, 96)]
+        for a, b in runs:
+            gtt(r("FD", a, b), r("TR"), r("LS", a // 16, b // 16), r("dif", a, b), A.mult)
+        for a, b in runs:
+            tt(r("M", a, b), r("FD", a, b), r("base", a, b), A.add)
+        for a, b in runs:
+            copy(r("Mc", a, b), r("M", a, b))
+        m3, m2, m1 = [slot("Mc", k) for k in range(3)]
+        if n == 1:
+            next_legs()
+            copy(r("Qc"), r("pland1"))
+            gboth("W0", "FP", r("Qc"))
+            gboth("W1", "W0", m3)
+            gboth("W0", "W1", m2)
+            gboth("W2", "W0", r("Qc"))
+            gboth("W1", "W2", m1)
+        else:
+            gboth("W0", "FP", m3)
+            gboth("W2", "W0", m2)
+            gboth("W1", "W2", m1)
+        gtt(r("FD", 96, 128), r("TR"), r("LS", 6, 8), r("dif", 96, 128), A.mult)
+        gtt(r("DM"), r("W1"), r("Rc"), r("mask"), A.mult)
+        if n < 3:
+            pn = r("pn" + me)
+            tt(pn, slot("FD", 3), slot("base", 3), A.add)
+            nxt = rank ^ MASKS[n]
+            landed(nxt, "aP%d" % (n + 1), [r("pland%d" % (n + 1))])
+            send(nxt, ap(r("pland%d" % (n + 1))), ap(pn), pn, "aP%d" % (n + 1))
+        scan(r("SC"), r("DM"))
+
+        def l4(t, a=0, b=24):
+            return r("l4", 24 * t + a, 24 * t + b)
+
+        def list4(t):
+            ts(l4(t), last("SC"), 4.0, float(t), A.mult, A.add)
+
+        def zpart(t, a, b):
+            gtt(r("z", 4 * a + t, 4 * b, 4), r("V", 384 * t, 384 * t + 384), r("Fc", a // 16, b // 16),
+                r("V2", 384 * t + a, 384 * t + b), A.add)
+
+        def twin(f, t):
+            f(r("V2", 384 * t, 384 * t + 384), r("V", 384 * t, 384 * t + 384))
+
+        def zquant(a, b):
+            quant(r("zq", a, b), r("zp", a, b), r("z", 4 * a, 4 * b))
+        list4(0)
+        list4(1)
+        ts(r("ki"), last("SC"), FRAC, None, A.mult)
+        gts(r("V", 0, 192), r("X"), l4(0, 0, 12), 0.5, A.mult)
+        ts(r("kk" + me), r("ki"), 4095, None, A.bitwise_and)
+        send(mate, ap(r("kland" + me)), ap(r("kk" + me, 0, 12)), r("kk" + me, 0, 12), "aK" + me)
+        gact(r("V", 192, 384), r("X"), l4(0, 12, 24), scale=0.5)
+        list4(2)
+        list4(3)
+        for t in (1, 2, 3):
+            gact(r("V", 384 * t, 384 * t + 384), r("X"), l4(t), scale=0.5)
+        twin(copy, 0)
+        for t in range(4):
+            if t < 2:
+                twin(copy, t + 1)
+            if t == 2:
+                twin(act, 3)
+            zpart(t, 0, CUT)
+        zquant(0, CUT)
+        for t in range(4):
+            zpart(t, CUT, 384)
+        zquant(CUT, 384)
+        copy(r("kc"), r("kk" + me, 12, 24))
+        if n < 3:
+            pl = r("pland%d" % (n + 1))
+            copy(r("Qc"), pl)
+            if n == 1:
+                quant(r("eq"), r("ep"), r("et"))
+        copy(r("kp"), r("kland" + me))
+        for p, a, c in (("psA", 0, CUT), ("psB", CUT, 384)):
+            for b in range(4):
+                o = ps(p, b, c - a)
+                mm(o, r("wq", 128 * b, 128 * b + 128), r("wp", 128 * b, 128 * b + 128), r("zq", a, c), r("zp", a, c))
+                act(r("H", 384 * b + a, 384 * b + c), o, scale=0.03125)
+        for b, c in ((0, 192), (1, 192), (2, 128), (3, 0)):
+            w = r("H", 384 * b, 384 * b + 384)
+            if c > 0:
+                gcopy(r("hs", b, 4 * c, 4), w, r("kp", 0, c // 16))
+        for b, c in ((3, 0), (2, 128)):
+            gact(r("hs", 4 * c + b, 768, 4), r("H", 384 * b, 384 * b + 384), r("kp", c // 16, 12))
+        quant(r("hq" + me), r("hp" + me), r("hs"))
+        send(mate, T["hlq" + me][:, 0:192].bitcast(dt.uint8), T["hq" + me][:, 0:192].bitcast(dt.uint8), r("hq" + me), "aH" + me)
+        send(mate, ap(r("hlp" + me)), ap(r("hp" + me)), r("hp" + me), "aH" + me)
+        if n < 3:
+            gact(r("Qw"), r("idw"), r("Qc"))
+            gact(r("Yw"), r("W1"), r("Rc"))
+            gact(r("G1"), r("Yw"), r("Fc"))
+        for b in range(4):
+            o = r("X", 768 + b, 1536, 4)
+            gtt(o, r("H", 384 * b, 384 * b + 384), r("kc"), o, A.add)
+        if n < 3:
+            scores(1, qx(1))
+            signs(1, "a")
+            gact(r("G2"), r("G1"), r("Fc"))
+            act(r("t1", 0, 24), slot("FD", 3), scale=-2.0)
+            act(slot("base", 1), pn)
+            act(slot("base", 3), pn)
+            act(slot("base", 0), pl)
+            act(slot("base", 2), pl)
+            gtt(r("DM2"), r("Qw"), r("Ec"), r("mask"), A.mult)
+            scan(r("SC2"), r("DM2"))
+            tt(slot("dif", 0), last("SC2"), pl, A.subtract)
+            tt(slot("dif", 2), last("SC2"), pl, A.subtract)
+            tt(slot("dif", 1), slot("dif", 1), r("t1", 0, 24), A.add)
+            tt(slot("dif", 3), slot("dif", 3), r("t1", 0, 24), A.add)
+            next_legs()
+        else:
+            def out(half, q):
+                a, b = 192 * half, 192 * half + 192
+                c, s = qx(half)
+                store("s", T.oc[:, 4 * a:4 * b], T.qx[:, a:b].bitcast(dt.uint8), c)
+                for k in range(4):
+                    store("a" if k % 2 else "s", T.osc[4 * k:4 * k + 4, a:b], T.qp[32 * k:32 * k + 4, a:b], s)
+                o = ps("psB", 2 + half, 192)
+                mm(o, r("vq"), r("vp"), c, s)
+                d = r("ys", a, b)
+                if q == "v":
+                    copy(d, o)
+                else:
+                    act(d, o)
+                store("s", T.y[:, a:b], ap(d), d)
+            quant(r("vq"), r("vp"), r("vb"))
+            out(1, "a")
+            tt(r("M", 96, 120), slot("FD", 3), slot("base", 3), A.add)
+            copy(r("Yc"), last("SC"))
+            copy(r("Pc"), r("M", 96, 120))
+            gact(r("yo"), r("idw"), r("Yc"))
+            gact(r("po"), r("idw"), r("Pc"))
+            store("s", T.pl[:, 0:384], T.yo[0:128:16, :], r("yo"))
+            store("a", T.pl[:, 384:768], T.po[0:128:16, :], r("po"))
+        for b in range(4):
+            o = ps("psA", b, 192)
+            mm(o, r("eq", 128 * b, 128 * b + 128), r("ep", 128 * b, 128 * b + 128), r("hlq" + me), r("hlp" + me))
+            d = r("X", b, 768, 4)
+            tt(d, o, d, A.add)
+    out(0, "v")
+    g.wait_ge(T.sem.snd, sent[0])
+    g.wait_ge(T.sem.stS, stores["s"])
+    g.wait_ge(T.sem.stA, stores["a"])
+    for q in ("g", "v", "a", "t"):
+        need("g", [("q" + q, count[q])])

@@ -2,6 +2,7 @@ from concourse.mybir import dt, AluOpType, ActivationFunctionType
 
 MASKS = [1, 2, 3]
 FRAC = 4096.0
+BIG = 2.0 ** 40
 CUT = 256
 
 _BF, _F32, _I32, _U16, _X4, _U8 = "bfloat16", "float32", "int32", "uint16", "float8_e4m3fn_x4", "uint8"
@@ -10,20 +11,22 @@ _SB = {
     "lgi": (24, _I32), "pbi": (24, _I32), "fdi": (24, _I32), "exi": (24, _I32),
     "wq": (512, _X4), "wp": (512, _U8), "uq": (128, _X4), "up": (128, _U8), "vq": (128, _X4), "vp": (128, _U8),
     "ones": (512, _BF), "et": (2048, _BF), "eq": (512, _X4), "ep": (512, _U8),
-    "idw": (384, _F32), "ids": (384, _F32), "mask": (384, _F32), "reset": (384, _BF), "FP": (384, _F32), "cq": (384, _F32),
-    "pi": (2, _I32), "ti": (16, _I32), "tf": (2, _F32), "lsi": (8, _F32), "LS": (8, _U16),
+    "idw": (384, _F32), "ids": (384, _F32), "hold": (384, _F32), "FP": (384, _F32), "cq": (16, _F32), "cm": (16, _F32), "c1": (16, _F32),
+    "c2": (16, _F32), "c3": (16, _F32), "Hc": (24, _U16), "e15": (2, _F32), "scl": (4, _F32),
+    "pi": (2, _I32), "ti": (16, _I32), "tf": (2, _F32), "PE": (24, _F32), "QE": (24, _F32), "F2": (384, _F32), "F3": (384, _F32),
+    "F3c": (24, _U16), "DR": (384, _F32), "lsi": (8, _F32), "LS": (8, _U16),
     "i16": (24, _F32), "pqi": (2, _I32), "pqf": (2, _F32), "idc": (24, _F32), "Emin": (24, _F32),
     "Fc": (24, _U16), "Yc": (24, _U16), "Ec": (24, _U16), "mE": (26, _U16), "Pc": (24, _U16), "Qc": (24, _U16),
     "base": (128, _F32), "dif": (128, _F32), "FD": (128, _F32), "M": (128, _F32), "Mc": (96, _U16), "Rc": (24, _U16),
-    "W0": (384, _F32), "W1": (384, _F32), "W2": (384, _F32), "Pw": (384, _F32), "Qw": (384, _F32), "Yw": (384, _F32),
+    "W0": (384, _F32), "W1": (384, _F32), "W2": (384, _F32), "Pw": (384, _F32), "Qw": (384, _F32), "Yw": (384, _F32), "DW": (384, _F32),
     "G1": (384, _F32), "G2": (384, _F32),
-    "DM": (384, _F32), "SC": (384, _F32), "DM2": (384, _F32), "SC2": (384, _F32), "DM3": (384, _F32), "SC3": (384, _F32),
-    "l4": (96, _U16), "ki": (24, _I32), "kc": (12, _U16), "kp": (12, _U16), "t1": (32, _F32),
+    "SC": (384, _F32), "DM2": (384, _F32), "SC2": (384, _F32), "DM3": (384, _F32), "SC3": (384, _F32),
+    "l4": (96, _U16), "ki": (24, _I32), "f3i": (24, _I32), "kc": (12, _U16), "kp": (12, _U16), "t1": (32, _F32),
     "V": (1536, _BF), "V2": (1536, _BF), "z": (1536, _BF), "H": (1536, _BF), "hs": (768, _BF),
     "zq": (384, _X4), "zp": (384, _U8), "qx": (384, _X4), "qp": (384, _U8),
     "rb": (384, _BF), "G": (400, _BF), "TR": (768, _BF),
     "ys": (384, _F32), "yo": (384, _F32), "po": (384, _F32),
-    "pn1": (24, _F32), "pn2": (24, _F32), "pland1": (24, _I32), "pland2": (24, _F32), "pland3": (24, _F32),
+    "pn1": (24, _F32), "pn2": (24, _F32), "pland1": (24, _U16), "pland2": (24, _F32), "pland3": (24, _F32),
 }
 for _n in (1, 2, 3):
     _SB["kk%d" % _n] = (24, _I32)
@@ -139,6 +142,9 @@ def rank_program(g, core, T, topo):
     def tsp(o, i, col, s2, *ops):
         op("v", lambda e: e.tensor_scalar(ap(o), ap(i), ap(col), s2, *ops), [i, col], [o])
 
+    def tsq(o, i, s1, col, *ops):
+        op("v", lambda e: e.tensor_scalar(ap(o), ap(i), s1, ap(col), *ops), [i, col], [o])
+
     def tt(o, i, j, f):
         op("v", lambda e: e.tensor_tensor(ap(o), ap(i), ap(j), f), [i, j], [o])
 
@@ -158,7 +164,7 @@ def rank_program(g, core, T, topo):
         op("v", lambda e: e.transpose(ap(o), ap(i)), [i], [o])
 
     def scan(o, i):
-        op("v", lambda e: e.tensor_tensor_scan(ap(o), ap(r("reset")), ap(i), 0.0, A.mult, A.add), [r("reset"), i], [o])
+        op("v", lambda e: e.tensor_tensor_scan(ap(o), ap(r("hold")), ap(i), 0.0, A.mult, A.subtract), [r("hold"), i], [o])
 
     def act(o, i, f=None, scale=1.0):
         op("a", lambda e: e.activation(ap(o), ap(i), F.Copy if f is None else f, scale=scale), [i], [o])
@@ -191,18 +197,26 @@ def rank_program(g, core, T, topo):
         eng[q].dma_start(o, i).then_inc(T.sem["stS" if q == "s" else "stA"], 16)
         stores[q] += 16
 
-    def send(to, o, i, v, sem):
+    def lanes(a, b, few):
+        e = topo.engines(a, b)
+        return e[::2] if few else e
+
+    def send(to, o, i, v, sem, few=False):
         need("g", deps("g", [v], []))
         dst = T.cores[to]
         rid, pid = topo.addr(dst)[:2]
-        g.remote_dma(o, i, T.sem[sem], T.sem.snd, pid, rid, topo.mask(core, dst))
-        sent[0] += len(topo.engines(core, dst))
+        e = lanes(core, dst, few)
+        g.remote_dma(o, i, T.sem[sem], T.sem.snd, pid, rid, sum(1 << k for k in e))
+        sent[0] += len(e)
 
-    def landed(frm, sem, views, calls=1):
-        arrived((sem, calls * len(topo.engines(T.cores[frm], core))), views)
+    def landed(frm, sem, views, calls=1, few=False):
+        arrived((sem, calls * len(lanes(T.cores[frm], core, few))), views)
 
     def last(n):
         return r(n, 15, 384, 16)
+
+    def scl(k):
+        return r("scl", k, k + 1)
 
     def slot(n, k):
         return r(n, 32 * k, 32 * k + 24)
@@ -218,21 +232,18 @@ def rank_program(g, core, T, topo):
     load("s", "ws", ap(r("wp")), T.ws[:, :], r("wp"))
     load("s", "v", ap(r("vb")), T.v[:, :], r("vb"))
     p1 = rank ^ MASKS[0]
-    landed(p1, "aP1", [r("pland1")])
+    landed(p1, "aP1", [r("pland1")], few=True)
 
     iota(r("pi"), [[0, 2]], 0, 1)
+    iota(r("i16"), [[16, 24]], 0, 0)
+    iota(r("cq"), [[1, 16]], 0, 0)
+    iota(r("cm"), [[1, 16]], -1, 0)
+    iota(r("idw"), [[1, 384]], 0, 0)
     iota(r("lsi", 0, 6), [[-1, 3], [256, 2]], 2, 0)
     iota(r("lsi", 6, 8), [[256, 2]], 3, 0)
-    iota(r("i16"), [[16, 24]], 0, 0)
-    iota(r("idw"), [[1, 384]], 0, 0)
-    iota(r("cq"), [[0, 24], [1, 16]], 0, 0)
-    send(p1, ap(r("pland1")), ap(r("pbi")), r("pbi"), "aP1")
     op("v", lambda e: e.memset(ap(r("ones")), 1.0), [], [r("ones")])
     op("v", lambda e: e.memset(ap(r("base")), 0.0), [], [r("base")])
     op("v", lambda e: e.memset(ap(r("dif")), 0.0), [], [r("dif")])
-    keep(r("reset"), r("ones", 0, 384), [[0, 24], [1, 16]], A.is_ge, -1, 0)
-    for b in range(4):
-        keep(r("et", 512 * b, 512 * b + 512), r("ones"), [[-1, 512]], A.is_equal, b, 4)
 
     def t1(k):
         return r("ti", k, k + 1)
@@ -240,6 +251,15 @@ def rank_program(g, core, T, topo):
     ts(pqi, pi, 15, None, A.bitwise_and)
     ts(t1(0), pi, 4, 1, A.logical_shift_right, A.bitwise_and)
     copy(pqf, pqi)
+    tsq(r("Hc"), r("i16"), 0.0, pqf, A.mult, A.add)
+    tsp(r("c1"), r("cq"), pqf, None, A.not_equal)
+    tsp(r("c2"), r("cm"), pqf, BIG, A.is_equal, A.mult)
+    ts(r("e15", 0, 1), pqf, 15.0, -1.0, A.is_equal, A.mult)
+    tt(r("c3"), r("c1"), r("c2"), A.add)
+    gact(r("hold"), r("c3"), r("Hc"))
+    ts(scl(0), r("e15", 0, 1), -1.0 / BIG, 1.0, A.add, A.mult)
+    ts(scl(1), r("e15", 0, 1), -1.0 / BIG, 4.0, A.add, A.mult)
+    ts(scl(2), r("e15", 0, 1), -1.0 / BIG, FRAC, A.add, A.mult)
     tt(t1(1), pi, t1(0), A.add)
     ts(t1(2), pqi, 0, 384, A.is_equal, A.mult)
     ts(t1(3), pqi, 16, None, A.mult)
@@ -249,16 +269,17 @@ def rank_program(g, core, T, topo):
     ts(t1(6), t1(4), 368, None, A.mult)
     tt(r("tf", 0, 1), t1(6), t1(3), A.add)
     tt(r("tf", 1, 2), r("tf", 0, 1), t1(5), A.add)
-    tsp(r("LS", 1, 8, 2), r("lsi", 1, 8, 2), r("tf", 0, 1), 767.0, A.add, A.min)
-    tsp(r("LS", 0, 8, 2), r("lsi", 0, 8, 2), r("tf", 1, 2), 767.0, A.add, A.min)
     act(r("ids"), r("idw"), scale=1.0 / FRAC)
-    act(slot("base", 0), r("idc"))
-    act(slot("base", 2), r("idc"))
 
     copy(r("Pc"), r("pbi"))
+    send(p1, ap(r("pland1")), ap(r("Pc")), r("Pc"), "aP1", few=True)
+    for b in range(4):
+        keep(r("et", 512 * b, 512 * b + 512), r("ones"), [[-1, 512]], A.is_equal, b, 4)
     copy(r("Yc"), r("lgi"))
     gact(r("Pw"), r("idw"), r("Pc"))
     gact(r("Yw"), r("idw"), r("Yc"))
+    act(slot("base", 0), r("idc"))
+    act(slot("base", 2), r("idc"))
     copy(r("Fc"), r("fdi"))
     tt(r("Emin"), r("exi"), r("idc"), A.min)
     copy(r("Ec"), r("exi"))
@@ -268,7 +289,8 @@ def rank_program(g, core, T, topo):
     copy(slot("base", 1), r("pbi"))
     gtt(r("FP"), r("ids"), r("Fc"), r("idw"), A.add)
     gact(r("G1"), r("Yw"), r("Fc"))
-    tsp(r("mask"), r("cq"), pqf, None, A.is_equal)
+    tsp(r("LS", 1, 8, 2), r("lsi", 1, 8, 2), r("tf", 0, 1), 767.0, A.add, A.min)
+    tsp(r("LS", 0, 8, 2), r("lsi", 0, 8, 2), r("tf", 1, 2), 767.0, A.add, A.min)
     quant(r("uq"), r("up"), r("ub"))
 
     def qx(half):
@@ -289,21 +311,17 @@ def rank_program(g, core, T, topo):
             act(d, o, F.Relu, -1.0)
 
     gact(r("G2"), r("G1"), r("Fc"))
+    gcopy(r("DM2"), r("Pw"), r("Ec"))
     scores(0, qx(0))
-    gtt(r("DM2"), r("Pw"), r("Ec"), r("mask"), A.mult)
-    scores(1, qx(1))
-    signs(0, "a")
-    signs(1, "a")
     scan(r("SC2"), r("DM2"))
-    act(slot("dif", 2), slot("dif", 0))
-    tt(slot("dif", 1), last("SC2"), slot("base", 1), A.subtract)
-    act(slot("base", 3), slot("base", 1))
-    act(slot("dif", 3), slot("dif", 1))
+    scores(1, qx(1))
+    signs(0, "v")
+    gact(r("DM3"), r("G2"), r("Fc"))
+    signs(1, "v")
 
-    def next_legs():
-        gtt(r("DM3"), r("G2"), r("Fc"), r("mask"), A.mult)
-        scan(r("SC3"), r("DM3"))
-        copy(r("Rc"), last("SC3"))
+    def short(o, i, w):
+        scan(w, i)
+        tsp(o, last(w[0]), scl(0), None, A.mult)
 
     for n in (1, 2, 3):
         me = str(n)
@@ -315,43 +333,50 @@ def rank_program(g, core, T, topo):
             signs(0, "v")
         gts(r("G", 0, 192), r("rb"), r("mE", 0, 12), 0.0, A.is_gt)
         gact(r("G", 192, 400), r("rb"), r("mE", 12, 25), F.Sign)
+        if n == 1:
+            tsp(r("PE"), last("SC2"), scl(0), None, A.mult)
+            tt(slot("dif", 1), r("PE"), slot("base", 1), A.subtract)
+            act(slot("dif", 2), slot("dif", 0))
+            act(slot("base", 3), slot("base", 1))
+            act(slot("dif", 3), slot("dif", 1))
+            gact(r("W0"), r("FP"), r("pland1"))
+            scan(r("SC3"), r("DM3"))
         turn(r("TR", 0, 384), r("G", 0, 384))
         turn(r("TR", 384, 768), r("G", 16, 400))
         runs = [(0, 32), (32, 96)]
         for a, b in runs:
             gtt(r("FD", a, b), r("TR"), r("LS", a // 16, b // 16), r("dif", a, b), A.mult)
+        if n == 1:
+            tsp(r("Rc"), last("SC3"), scl(0), None, A.mult)
         for a, b in runs:
             tt(r("M", a, b), r("FD", a, b), r("base", a, b), A.add)
         for a, b in runs:
             copy(r("Mc", a, b), r("M", a, b))
         m3, m2, m1 = [slot("Mc", k) for k in range(3)]
         if n == 1:
-            next_legs()
-            copy(r("Qc"), r("pland1"))
-            gboth("W0", "FP", r("Qc"))
             gboth("W1", "W0", m3)
             gboth("W0", "W1", m2)
-            gboth("W2", "W0", r("Qc"))
+            gboth("W2", "W0", r("pland1"))
             gboth("W1", "W2", m1)
         else:
             gboth("W0", "FP", m3)
             gboth("W2", "W0", m2)
             gboth("W1", "W2", m1)
         gtt(r("FD", 96, 128), r("TR"), r("LS", 6, 8), r("dif", 96, 128), A.mult)
-        gtt(r("DM"), r("W1"), r("Rc"), r("mask"), A.mult)
+        gboth("DW", "W1", r("Rc"))
         if n < 3:
             pn = r("pn" + me)
             tt(pn, slot("FD", 3), slot("base", 3), A.add)
             nxt = rank ^ MASKS[n]
             landed(nxt, "aP%d" % (n + 1), [r("pland%d" % (n + 1))])
             send(nxt, ap(r("pland%d" % (n + 1))), ap(pn), pn, "aP%d" % (n + 1))
-        scan(r("SC"), r("DM"))
+        scan(r("SC"), r("DW"))
 
         def l4(t, a=0, b=24):
             return r("l4", 24 * t + a, 24 * t + b)
 
         def list4(t):
-            ts(l4(t), last("SC"), 4.0, float(t), A.mult, A.add)
+            tsp(l4(t), last("SC"), scl(1), float(t), A.mult, A.add)
 
         def zpart(t, a, b):
             gtt(r("z", 4 * a + t, 4 * b, 4), r("V", 384 * t, 384 * t + 384), r("Fc", a // 16, b // 16),
@@ -364,70 +389,83 @@ def rank_program(g, core, T, topo):
             quant(r("zq", a, b), r("zp", a, b), r("z", 4 * a, 4 * b))
         list4(0)
         list4(1)
-        ts(r("ki"), last("SC"), FRAC, None, A.mult)
-        gts(r("V", 0, 192), r("X"), l4(0, 0, 12), 0.5, A.mult)
+        tsp(r("ki"), last("SC"), scl(2), None, A.mult)
+        gts(r("V", 0, 320), r("X"), l4(0, 0, 20), 0.5, A.mult)
         ts(r("kk" + me), r("ki"), 4095, None, A.bitwise_and)
         send(mate, ap(r("kland" + me)), ap(r("kk" + me, 0, 12)), r("kk" + me, 0, 12), "aK" + me)
-        gact(r("V", 192, 384), r("X"), l4(0, 12, 24), scale=0.5)
+        gact(r("V", 320, 384), r("X"), l4(0, 20, 24), scale=0.5)
         list4(2)
         list4(3)
         for t in (1, 2, 3):
             gact(r("V", 384 * t, 384 * t + 384), r("X"), l4(t), scale=0.5)
+        twin(act, 3)
+        if n == 1:
+            gact(r("F2"), r("FP"), r("Fc"))
+            gact(r("F3"), r("F2"), r("Fc"))
+        if n == 2:
+            gact(r("DR"), r("DW"), r("F3c"))
         twin(copy, 0)
-        for t in range(4):
-            if t < 2:
-                twin(copy, t + 1)
-            if t == 2:
-                twin(act, 3)
-            zpart(t, 0, CUT)
+        twin(copy, 1)
+        zpart(0, 0, CUT)
+        twin(copy, 2)
+        zpart(1, 0, CUT)
+        zpart(2, 0, CUT)
+        zpart(3, 0, CUT)
         zquant(0, CUT)
         for t in range(4):
             zpart(t, CUT, 384)
         zquant(CUT, 384)
         copy(r("kc"), r("kk" + me, 12, 24))
-        if n < 3:
-            pl = r("pland%d" % (n + 1))
-            copy(r("Qc"), pl)
-            if n == 1:
-                quant(r("eq"), r("ep"), r("et"))
+        if n == 1:
+            quant(r("eq", 0, 256), r("ep", 0, 256), r("et", 0, 1024))
+        if n == 2:
+            short(r("Rc"), r("DR"), r("SC3"))
         copy(r("kp"), r("kland" + me))
         for p, a, c in (("psA", 0, CUT), ("psB", CUT, 384)):
             for b in range(4):
                 o = ps(p, b, c - a)
                 mm(o, r("wq", 128 * b, 128 * b + 128), r("wp", 128 * b, 128 * b + 128), r("zq", a, c), r("zp", a, c))
                 act(r("H", 384 * b + a, 384 * b + c), o, scale=0.03125)
-        for b, c in ((0, 192), (1, 192), (2, 128), (3, 0)):
-            w = r("H", 384 * b, 384 * b + 384)
-            if c > 0:
-                gcopy(r("hs", b, 4 * c, 4), w, r("kp", 0, c // 16))
-        for b, c in ((3, 0), (2, 128)):
-            gact(r("hs", 4 * c + b, 768, 4), r("H", 384 * b, 384 * b + 384), r("kp", c // 16, 12))
+        for b in range(4):
+            f = gact if b == 3 else gcopy
+            f(r("hs", b, 768, 4), r("H", 384 * b, 384 * b + 384), r("kp"))
         quant(r("hq" + me), r("hp" + me), r("hs"))
         send(mate, T["hlq" + me][:, 0:192].bitcast(dt.uint8), T["hq" + me][:, 0:192].bitcast(dt.uint8), r("hq" + me), "aH" + me)
         send(mate, ap(r("hlp" + me)), ap(r("hp" + me)), r("hp" + me), "aH" + me)
         if n < 3:
+            pl = r("pland%d" % (n + 1))
+            copy(r("Qc"), pl)
             gact(r("Qw"), r("idw"), r("Qc"))
-            gact(r("Yw"), r("W1"), r("Rc"))
-            gact(r("G1"), r("Yw"), r("Fc"))
+            gact(r("DM2"), r("Qw"), r("Ec"))
+            if n == 1:
+                scan(r("SC3"), r("F3"))
+                tsp(r("ki"), last("SC3"), scl(2), None, A.mult)
+                ts(r("f3i"), r("ki"), 4095, None, A.bitwise_and)
+                copy(r("F3c"), r("f3i"))
+                gact(r("DR"), r("DW"), r("F3c"))
         for b in range(4):
             o = r("X", 768 + b, 1536, 4)
             gtt(o, r("H", 384 * b, 384 * b + 384), r("kc"), o, A.add)
         if n < 3:
             scores(1, qx(1))
             signs(1, "a")
-            gact(r("G2"), r("G1"), r("Fc"))
             act(r("t1", 0, 24), slot("FD", 3), scale=-2.0)
             act(slot("base", 1), pn)
             act(slot("base", 3), pn)
             act(slot("base", 0), pl)
             act(slot("base", 2), pl)
-            gtt(r("DM2"), r("Qw"), r("Ec"), r("mask"), A.mult)
             scan(r("SC2"), r("DM2"))
-            tt(slot("dif", 0), last("SC2"), pl, A.subtract)
-            tt(slot("dif", 2), last("SC2"), pl, A.subtract)
+            if n == 1:
+                scan(r("SC3"), r("DR"))
+            tsp(r("QE"), last("SC2"), scl(0), None, A.mult)
+            if n == 1:
+                tsp(r("Rc"), last("SC3"), scl(0), None, A.mult)
+            tt(slot("dif", 0), r("QE"), pl, A.subtract)
+            tt(slot("dif", 2), r("QE"), pl, A.subtract)
             tt(slot("dif", 1), slot("dif", 1), r("t1", 0, 24), A.add)
             tt(slot("dif", 3), slot("dif", 3), r("t1", 0, 24), A.add)
-            next_legs()
+            if n == 1:
+                quant(r("eq", 256, 512), r("ep", 256, 512), r("et", 1024, 2048))
         else:
             def out(half, q):
                 a, b = 192 * half, 192 * half + 192
@@ -446,7 +484,7 @@ def rank_program(g, core, T, topo):
             quant(r("vq"), r("vp"), r("vb"))
             out(1, "a")
             tt(r("M", 96, 120), slot("FD", 3), slot("base", 3), A.add)
-            copy(r("Yc"), last("SC"))
+            tsp(r("Yc"), last("SC"), scl(0), None, A.mult)
             copy(r("Pc"), r("M", 96, 120))
             gact(r("yo"), r("idw"), r("Yc"))
             gact(r("po"), r("idw"), r("Pc"))

from concourse.mybir import dt, AluOpType, ActivationFunctionType

MASKS = [1, 2, 3]
FRAC = 4096.0
BIG = 2.0 ** 40
CUT = 256

_BF, _F32, _I32, _U16, _X4, _U8 = "bfloat16", "float32", "int32", "uint16", "float8_e4m3fn_x4", "uint8"
_SB = {
    "X": (1536, _BF), "ub": (512, _BF), "vb": (512, _BF),
    "lgi": (24, _I32), "pbi": (24, _I32), "fdi": (24, _I32), "exi": (24, _I32),
    "wq": (512, _X4), "wp": (512, _U8), "uq": (128, _X4), "up": (128, _U8), "vq": (128, _X4), "vp": (128, _U8),
    "ones": (512, _BF), "et": (2048, _BF), "eq": (512, _X4), "ep": (512, _U8),
    "idw": (384, _F32), "ids": (384, _F32), "hold": (384, _F32), "FP": (384, _F32), "cq": (16, _F32), "cm": (16, _F32), "c1": (16, _F32),
    "c2": (16, _F32), "c3": (16, _F32), "Hc": (24, _U16), "e15": (2, _F32), "scl": (4, _F32),
    "pi": (2, _I32), "ti": (16, _I32), "tf": (2, _F32), "PE": (24, _F32), "QE": (24, _F32), "F2": (384, _F32), "F3": (384, _F32),
    "F3c": (24, _U16), "DR": (384, _F32), "lsi": (8, _F32), "LS": (8, _U16),
    "i16": (24, _F32), "pqi": (2, _I32), "pqf": (2, _F32), "idc": (24, _F32), "Emin": (24, _F32),
    "Fc": (24, _U16), "Yc": (24, _U16), "Ec": (24, _U16), "mE": (26, _U16), "Pc": (24, _U16), "Qc": (24, _U16),
    "base": (128, _F32), "dif": (128, _F32), "FD": (128, _F32), "M": (128, _F32), "Mc": (96, _U16), "Rc": (24, _U16),
    "W0": (384, _F32), "W1": (384, _F32), "W2": (384, _F32), "Pw": (384, _F32), "Qw": (384, _F32), "Yw": (384, _F32), "DW": (384, _F32),
    "G1": (384, _F32), "G2": (384, _F32),
    "SC": (384, _F32), "DM2": (384, _F32), "SC2": (384, _F32), "DM3": (384, _F32), "SC3": (384, _F32),
    "l4": (96, _U16), "ki": (24, _I32), "f3i": (24, _I32), "kc": (12, _U16), "kp": (12, _U16), "t1": (32, _F32),
    "V": (1536, _BF), "V2": (1536, _BF), "z": (1536, _BF), "H": (1536, _BF), "hs": (768, _BF),
    "zq": (384, _X4), "zp": (384, _U8), "qx": (384, _X4), "qp": (384, _U8),
    "rb": (384, _BF), "G": (400, _BF), "TR": (768, _BF),
    "ys": (384, _F32), "yo": (384, _F32), "po": (384, _F32),
    "pn1": (24, _F32), "pn2": (24, _F32), "pland1": (24, _U16), "pland2": (24, _F32), "pland3": (24, _F32),
}
for _n in (1, 2, 3):
    _SB["kk%d" % _n] = (24, _I32)
    _SB["kland%d" % _n] = (12, _I32)
    _SB["hq%d" % _n] = (192, _X4)
    _SB["hp%d" % _n] = (192, _U8)
    _SB["hlq%d" % _n] = (192, _X4)
    _SB["hlp%d" % _n] = (192, _U8)
SCRATCH = {k: ("sbuf", [128, n], d) for k, (n, d) in _SB.items()}
SCRATCH["psA"] = ("psum", [128, 2048], "float32")
SCRATCH["psB"] = ("psum", [128, 2048], "float32")
SEMAPHORES = (["qg", "qv", "qa", "qt", "snd", "stS", "stA"]
              + ["ld_" + k for k in ("x0", "x1", "u", "v", "lg", "pb", "fd", "ex", "wc", "ws")]
              + ["%s%d" % (k, n) for k in ("aP", "aK", "aH") for n in (1, 2, 3)])


def r(name, lo=0, hi=None, step=1):
    return (name, lo, _SB[name][0] if hi is None else hi, step)


def ps(name, bank, n):
    return (name, 512 * bank, 512 * bank + n, 1)


def region(v):
    if v[0] in ("psA", "psB"):
        return (v[0], v[1] - v[1] % 512, v[1] - v[1] % 512 + 512, 1)
    return v


def meet(a, b):
    if a[1] >= b[2] or b[1] >= a[2]:
        return False
    return not (a[3] > 1 and a[3] == b[3] and a[1] % a[3] != b[1] % b[3])


def covers(a, b):
    return a[1] <= b[1] and b[2] <= a[2] and (a[3] == 1 or (a[3] == b[3] and a[1] % a[3] == b[1] % b[3]))


def machine(g, T):
    eng = {"g": g, "v": g.vector, "a": g.scalar, "t": g.tensor, "s": g.sync}
    count, seen, snap, log = {q: 0 for q in eng}, {q: {} for q in eng}, {}, {}

    def need(q, toks):
        want = {}
        for s, n in toks:
            if seen[q].get(s, 0) < n:
                want[s] = max(n, want.get(s, 0))
        for s in sorted(want):
            n = want[s]
            if any(o != s and snap.get((o, m), {}).get(s, 0) >= n for o, m in want.items()):
                continue
            eng[q].wait_ge(T.sem[s], n)
            seen[q][s] = max(n, seen[q].get(s, 0))
            for k, m in snap.get((s, n), {}).items():
                seen[q][k] = max(m, seen[q].get(k, 0))

    def deps(q, reads, writes):
        toks = []
        for v in [region(x) for x in reads]:
            bank = v[0] in ("psA", "psB")
            for w, kind, oq, tok in log.get(v[0], []):
                if meet(v, w) and (kind == "w" or (bank and oq != q)):
                    toks.append(tok)
        for v in [region(x) for x in writes]:
            for w, kind, oq, tok in log.get(v[0], []):
                if meet(v, w) and (kind == "w" or oq != q):
                    toks.append(tok)
        return toks

    def note(q, reads, writes, tok):
        for v in [region(x) for x in writes]:
            log[v[0]] = [e for e in log.get(v[0], []) if not covers(v, e[0])] + [(v, "w", q, tok)]
        for v in [region(x) for x in reads]:
            log.setdefault(v[0], []).append((v, "r", q, tok))

    def op(q, call, reads, writes):
        need(q, deps(q, reads, writes))
        count[q] += 1
        tok = ("q" + q, count[q])
        snap[tok] = dict(seen[q])
        call(eng[q]).then_inc(T.sem[tok[0]], 1)
        note(q, reads, writes, tok)

    def arrived(tok, writes):
        note("", [], writes, tok)

    return eng, op, need, deps, arrived, count


def rank_program(g, core, T, topo):
    rank = T.rank_of(core)
    if rank is None:
        return
    A, F = AluOpType, ActivationFunctionType
    eng, op, need, deps, arrived, count = machine(g, T)
    sent, stores = [0], {"s": 0, "a": 0}

    def ap(v):
        t = T[v[0]]
        return t[:, v[1]:v[2]] if v[3] == 1 else t[:, v[1]:v[2]:v[3]]

    def ind(w, o):
        return ap(w).indirect(ap(o))

    def copy(o, i):
        op("v", lambda e: e.tensor_copy(ap(o), ap(i)), [i], [o])

    def ts(o, i, s1, s2, *ops):
        op("v", lambda e: e.tensor_scalar(ap(o), ap(i), s1, s2, *ops), [i], [o])

    def tsp(o, i, col, s2, *ops):
        op("v", lambda e: e.tensor_scalar(ap(o), ap(i), ap(col), s2, *ops), [i, col], [o])

    def tsq(o, i, s1, col, *ops):
        op("v", lambda e: e.tensor_scalar(ap(o), ap(i), s1, ap(col), *ops), [i, col], [o])

    def tt(o, i, j, f):
        op("v", lambda e: e.tensor_tensor(ap(o), ap(i), ap(j), f), [i, j], [o])

    def gtt(o, w, l, j, f):
        op("v", lambda e: e.tensor_tensor(ap(o), ind(w, l), ap(j), f), [w, l, j], [o])

    def gts(o, w, l, s1, f):
        op("v", lambda e: e.tensor_scalar(ap(o), ind(w, l), s1, None, f), [w, l], [o])

    def gcopy(o, w, l):
        op("v", lambda e: e.tensor_copy(ap(o), ind(w, l)), [w, l], [o])

    def quant(c, s, t):
        op("v", lambda e: e.quantize_mx(ap(c), ap(s), ap(t)), [t], [c, s])

    def turn(o, i):
        op("v", lambda e: e.transpose(ap(o), ap(i)), [i], [o])

    def scan(o, i):
        op("v", lambda e: e.tensor_tensor_scan(ap(o), ap(r("hold")), ap(i), 0.0, A.mult, A.subtract), [r("hold"), i], [o])

    def act(o, i, f=None, scale=1.0):
        op("a", lambda e: e.activation(ap(o), ap(i), F.Copy if f is None else f, scale=scale), [i], [o])

    def gact(o, w, l, f=None, scale=1.0):
        op("a", lambda e: e.activation(ap(o), ind(w, l), F.Copy if f is None else f, scale=scale), [w, l], [o])

    def mm(o, lc, ls, rc, rs):
        op("t", lambda e: e.matmul_mx(ap(o), ap(lc), ap(ls), ap(rc), ap(rs), True, True), [lc, ls, rc, rs], [o])

    def gboth(o, w, l):
        gcopy(r(o, 0, 192), r(w), (l[0], l[1], l[1] + 12, 1))
        gact(r(o, 192, 384), r(w), (l[0], l[1] + 12, l[1] + 24, 1))

    def iota(o, pattern, base, cm):
        if _SB[o[0]][1] == _F32:
            op("g", lambda e: e.iota(ap(o), pattern, base, cm, allow_small_or_imprecise_dtypes=True), [], [o])
        else:
            op("g", lambda e: e.iota(ap(o), pattern, base, cm), [], [o])

    def keep(o, i, pattern, f, base, cm):
        op("g", lambda e: e.affine_select(ap(o), ap(i), pattern, f, 0.0, base, cm), [i], [o])

    def load(q, sem, o, src, v):
        eng[q].dma_start(o, src).then_inc(T.sem["ld_" + sem], 16)
        arrived(("ld_" + sem, 16), [v])

    def store(q, o, i, v):
        need(q, deps(q, [v], []))
        eng[q].dma_start(o, i).then_inc(T.sem["stS" if q == "s" else "stA"], 16)
        stores[q] += 16

    def lanes(a, b, few):
        e = topo.engines(a, b)
        return e[::2] if few else e

    def send(to, o, i, v, sem, few=False):
        need("g", deps("g", [v], []))
        dst = T.cores[to]
        rid, pid = topo.addr(dst)[:2]
        e = lanes(core, dst, few)
        g.remote_dma(o, i, T.sem[sem], T.sem.snd, pid, rid, sum(1 << k for k in e))
        sent[0] += len(e)

    def landed(frm, sem, views, calls=1, few=False):
        arrived((sem, calls * len(lanes(T.cores[frm], core, few))), views)

    def last(n):
        return r(n, 15, 384, 16)

    def scl(k):
        return r("scl", k, k + 1)

    def slot(n, k):
        return r(n, 32 * k, 32 * k + 24)

    load("s", "pb", ap(r("pbi")), T.pb[:, :], r("pbi"))
    load("s", "ex", ap(r("exi")), T.ex[:, :], r("exi"))
    load("a", "fd", ap(r("fdi")), T.fd[:, :], r("fdi"))
    load("a", "lg", ap(r("lgi")), T.lg[:, :], r("lgi"))
    load("s", "x0", ap(r("X", 0, 768)), T.x[:, 0:768], r("X", 0, 768))
    load("a", "u", ap(r("ub")), T.u[:, :], r("ub"))
    load("s", "x1", ap(r("X", 768, 1536)), T.x[:, 768:1536], r("X", 768, 1536))
    load("s", "wc", T.wq[:, :].bitcast(dt.uint8), T.wc[:, :], r("wq"))
    load("s", "ws", ap(r("wp")), T.ws[:, :], r("wp"))
    load("s", "v", ap(r("vb")), T.v[:, :], r("vb"))
    p1 = rank ^ MASKS[0]
    landed(p1, "aP1", [r("pland1")], few=True)

    iota(r("pi"), [[0, 2]], 0, 1)
    iota(r("i16"), [[16, 24]], 0, 0)
    iota(r("cq"), [[1, 16]], 0, 0)
    iota(r("cm"), [[1, 16]], -1, 0)
    iota(r("idw"), [[1, 384]], 0, 0)
    iota(r("lsi", 0, 6), [[-1, 3], [256, 2]], 2, 0)
    iota(r("lsi", 6, 8), [[256, 2]], 3, 0)
    op("v", lambda e: e.memset(ap(r("ones")), 1.0), [], [r("ones")])
    op("v", lambda e: e.memset(ap(r("base")), 0.0), [], [r("base")])
    op("v", lambda e: e.memset(ap(r("dif")), 0.0), [], [r("dif")])

    def t1(k):
        return r("ti", k, k + 1)
    pi, pqi, pqf = r("pi", 0, 1), r("pqi", 0, 1), r("pqf", 0, 1)
    ts(pqi, pi, 15, None, A.bitwise_and)
    ts(t1(0), pi, 4, 1, A.logical_shift_right, A.bitwise_and)
    copy(pqf, pqi)
    tsq(r("Hc"), r("i16"), 0.0, pqf, A.mult, A.add)
    tsp(r("c1"), r("cq"), pqf, None, A.not_equal)
    tsp(r("c2"), r("cm"), pqf, BIG, A.is_equal, A.mult)
    ts(r("e15", 0, 1), pqf, 15.0, -1.0, A.is_equal, A.mult)
    tt(r("c3"), r("c1"), r("c2"), A.add)
    gact(r("hold"), r("c3"), r("Hc"))
    ts(scl(0), r("e15", 0, 1), -1.0 / BIG, 1.0, A.add, A.mult)
    ts(scl(1), r("e15", 0, 1), -1.0 / BIG, 4.0, A.add, A.mult)
    ts(scl(2), r("e15", 0, 1), -1.0 / BIG, FRAC, A.add, A.mult)
    tt(t1(1), pi, t1(0), A.add)
    ts(t1(2), pqi, 0, 384, A.is_equal, A.mult)
    ts(t1(3), pqi, 16, None, A.mult)
    ts(t1(4), t1(1), 1, None, A.bitwise_and)
    tt(t1(5), t1(2), t1(0), A.mult)
    tsp(r("idc"), r("i16"), pqf, None, A.add)
    ts(t1(6), t1(4), 368, None, A.mult)
    tt(r("tf", 0, 1), t1(6), t1(3), A.add)
    tt(r("tf", 1, 2), r("tf", 0, 1), t1(5), A.add)
    act(r("ids"), r("idw"), scale=1.0 / FRAC)

    copy(r("Pc"), r("pbi"))
    send(p1, ap(r("pland1")), ap(r("Pc")), r("Pc"), "aP1", few=True)
    for b in range(4):
        keep(r("et", 512 * b, 512 * b + 512), r("ones"), [[-1, 512]], A.is_equal, b, 4)
    copy(r("Yc"), r("lgi"))
    gact(r("Pw"), r("idw"), r("Pc"))
    gact(r("Yw"), r("idw"), r("Yc"))
    act(slot("base", 0), r("idc"))
    act(slot("base", 2), r("idc"))
    copy(r("Fc"), r("fdi"))
    tt(r("Emin"), r("exi"), r("idc"), A.min)
    copy(r("Ec"), r("exi"))
    tt(slot("dif", 0), r("exi"), r("idc"), A.subtract)
    copy(r("mE", 0, 24), r("Emin"))
    copy(r("mE", 24, 25), r("Emin", 0, 1))
    copy(slot("base", 1), r("pbi"))
    gtt(r("FP"), r("ids"), r("Fc"), r("idw"), A.add)
    gact(r("G1"), r("Yw"), r("Fc"))
    tsp(r("LS", 1, 8, 2), r("lsi", 1, 8, 2), r("tf", 0, 1), 767.0, A.add, A.min)
    tsp(r("LS", 0, 8, 2), r("lsi", 0, 8, 2), r("tf", 1, 2), 767.0, A.add, A.min)
    quant(r("uq"), r("up"), r("ub"))

    def qx(half):
        c = r("qx", 192 * half, 192 * half + 192)
        s = r("qp", 192 * half, 192 * half + 192)
        quant(c, s, r("X", 768 * half, 768 * half + 768))
        return c, s

    def scores(half, cs):
        mm(ps("psB", half, 192), r("uq"), r("up"), cs[0], cs[1])

    def signs(half, q):
        o = ps("psB", half, 192)
        d = r("rb", 192 * half, 192 * half + 192)
        if q == "v":
            ts(d, o, -1.0, 0.0, A.mult, A.max)
        else:
            act(d, o, F.Relu, -1.0)

    gact(r("G2"), r("G1"), r("Fc"))
    gcopy(r("DM2"), r("Pw"), r("Ec"))
    scores(0, qx(0))
    scan(r("SC2"), r("DM2"))
    scores(1, qx(1))
    signs(0, "v")
    gact(r("DM3"), r("G2"), r("Fc"))
    signs(1, "v")

    def short(o, i, w):
        scan(w, i)
        tsp(o, last(w[0]), scl(0), None, A.mult)

    for n in (1, 2, 3):
        me = str(n)
        mate = rank ^ MASKS[n - 1]
        landed(mate, "aK" + me, [r("kland" + me)])
        landed(mate, "aH" + me, [r("hlq" + me), r("hlp" + me)], 2)
        if n > 1:
            scores(0, qx(0))
            signs(0, "v")
        gts(r("G", 0, 192), r("rb"), r("mE", 0, 12), 0.0, A.is_gt)
        gact(r("G", 192, 400), r("rb"), r("mE", 12, 25), F.Sign)
        if n == 1:
            tsp(r("PE"), last("SC2"), scl(0), None, A.mult)
            tt(slot("dif", 1), r("PE"), slot("base", 1), A.subtract)
            act(slot("dif", 2), slot("dif", 0))
            act(slot("base", 3), slot("base", 1))
            act(slot("dif", 3), slot("dif", 1))
            gact(r("W0"), r("FP"), r("pland1"))
            scan(r("SC3"), r("DM3"))
        turn(r("TR", 0, 384), r("G", 0, 384))
        turn(r("TR", 384, 768), r("G", 16, 400))
        runs = [(0, 32), (32, 96)]
        for a, b in runs:
            gtt(r("FD", a, b), r("TR"), r("LS", a // 16, b // 16), r("dif", a, b), A.mult)
        if n == 1:
            tsp(r("Rc"), last("SC3"), scl(0), None, A.mult)
        for a, b in runs:
            tt(r("M", a, b), r("FD", a, b), r("base", a, b), A.add)
        for a, b in runs:
            copy(r("Mc", a, b), r("M", a, b))
        m3, m2, m1 = [slot("Mc", k) for k in range(3)]
        if n == 1:
            gboth("W1", "W0", m3)
            gboth("W0", "W1", m2)
            gboth("W2", "W0", r("pland1"))
            gboth("W1", "W2", m1)
        else:
            gboth("W0", "FP", m3)
            gboth("W2", "W0", m2)
            gboth("W1", "W2", m1)
        gtt(r("FD", 96, 128), r("TR"), r("LS", 6, 8), r("dif", 96, 128), A.mult)
        gboth("DW", "W1", r("Rc"))
        if n < 3:
            pn = r("pn" + me)
            tt(pn, slot("FD", 3), slot("base", 3), A.add)
            nxt = rank ^ MASKS[n]
            landed(nxt, "aP%d" % (n + 1), [r("pland%d" % (n + 1))])
            send(nxt, ap(r("pland%d" % (n + 1))), ap(pn), pn, "aP%d" % (n + 1))
        scan(r("SC"), r("DW"))

        def l4(t, a=0, b=24):
            return r("l4", 24 * t + a, 24 * t + b)

        def list4(t):
            tsp(l4(t), last("SC"), scl(1), float(t), A.mult, A.add)

        def zpart(t, a, b):
            gtt(r("z", 4 * a + t, 4 * b, 4), r("V", 384 * t, 384 * t + 384), r("Fc", a // 16, b // 16),
                r("V2", 384 * t + a, 384 * t + b), A.add)

        def twin(f, t):
            f(r("V2", 384 * t, 384 * t + 384), r("V", 384 * t, 384 * t + 384))

        def zquant(a, b):
            quant(r("zq", a, b), r("zp", a, b), r("z", 4 * a, 4 * b))
        list4(0)
        list4(1)
        tsp(r("ki"), last("SC"), scl(2), None, A.mult)
        gts(r("V", 0, 320), r("X"), l4(0, 0, 20), 0.5, A.mult)
        ts(r("kk" + me), r("ki"), 4095, None, A.bitwise_and)
        send(mate, ap(r("kland" + me)), ap(r("kk" + me, 0, 12)), r("kk" + me, 0, 12), "aK" + me)
        gact(r("V", 320, 384), r("X"), l4(0, 20, 24), scale=0.5)
        list4(2)
        list4(3)
        for t in (1, 2, 3):
            gact(r("V", 384 * t, 384 * t + 384), r("X"), l4(t), scale=0.5)
        twin(act, 3)
        if n == 1:
            gact(r("F2"), r("FP"), r("Fc"))
            gact(r("F3"), r("F2"), r("Fc"))
        if n == 2:
            gact(r("DR"), r("DW"), r("F3c"))
        twin(copy, 0)
        twin(copy, 1)
        zpart(0, 0, CUT)
        twin(copy, 2)
        zpart(1, 0, CUT)
        zpart(2, 0, CUT)
        zpart(3, 0, CUT)
        zquant(0, CUT)
        for t in range(4):
            zpart(t, CUT, 384)
        zquant(CUT, 384)
        copy(r("kc"), r("kk" + me, 12, 24))
        if n == 1:
            quant(r("eq", 0, 256), r("ep", 0, 256), r("et", 0, 1024))
        if n == 2:
            short(r("Rc"), r("DR"), r("SC3"))
        copy(r("kp"), r("kland" + me))
        for p, a, c in (("psA", 0, CUT), ("psB", CUT, 384)):
            for b in range(4):
                o = ps(p, b, c - a)
                mm(o, r("wq", 128 * b, 128 * b + 128), r("wp", 128 * b, 128 * b + 128), r("zq", a, c), r("zp", a, c))
                act(r("H", 384 * b + a, 384 * b + c), o, scale=0.03125)
        for b in range(4):
            f = gact if b == 3 else gcopy
            f(r("hs", b, 768, 4), r("H", 384 * b, 384 * b + 384), r("kp"))
        quant(r("hq" + me), r("hp" + me), r("hs"))
        send(mate, T["hlq" + me][:, 0:192].bitcast(dt.uint8), T["hq" + me][:, 0:192].bitcast(dt.uint8), r("hq" + me), "aH" + me)
        send(mate, ap(r("hlp" + me)), ap(r("hp" + me)), r("hp" + me), "aH" + me)
        if n < 3:
            pl = r("pland%d" % (n + 1))
            copy(r("Qc"), pl)
            gact(r("Qw"), r("idw"), r("Qc"))
            gact(r("DM2"), r("Qw"), r("Ec"))
            if n == 1:
                scan(r("SC3"), r("F3"))
                tsp(r("ki"), last("SC3"), scl(2), None, A.mult)
                ts(r("f3i"), r("ki"), 4095, None, A.bitwise_and)
                copy(r("F3c"), r("f3i"))
                gact(r("DR"), r("DW"), r("F3c"))
        for b in range(4):
            o = r("X", 768 + b, 1536, 4)
            gtt(o, r("H", 384 * b, 384 * b + 384), r("kc"), o, A.add)
        if n < 3:
            scores(1, qx(1))
            signs(1, "a")
            act(r("t1", 0, 24), slot("FD", 3), scale=-2.0)
            act(slot("base", 1), pn)
            act(slot("base", 3), pn)
            act(slot("base", 0), pl)
            act(slot("base", 2), pl)
            scan(r("SC2"), r("DM2"))
            if n == 1:
                scan(r("SC3"), r("DR"))
            tsp(r("QE"), last("SC2"), scl(0), None, A.mult)
            if n == 1:
                tsp(r("Rc"), last("SC3"), scl(0), None, A.mult)
            tt(slot("dif", 0), r("QE"), pl, A.subtract)
            tt(slot("dif", 2), r("QE"), pl, A.subtract)
            tt(slot("dif", 1), slot("dif", 1), r("t1", 0, 24), A.add)
            tt(slot("dif", 3), slot("dif", 3), r("t1", 0, 24), A.add)
            if n == 1:
                quant(r("eq", 256, 512), r("ep", 256, 512), r("et", 1024, 2048))
        else:
            def out(half, q):
                a, b = 192 * half, 192 * half + 192
                c, s = qx(half)
                store("s", T.oc[:, 4 * a:4 * b], T.qx[:, a:b].bitcast(dt.uint8), c)
                for k in range(4):
                    store("a" if k % 2 else "s", T.osc[4 * k:4 * k + 4, a:b], T.qp[32 * k:32 * k + 4, a:b], s)
                o = ps("psB", 2 + half, 192)
                mm(o, r("vq"), r("vp"), c, s)
                d = r("ys", a, b)
                if q == "v":
                    copy(d, o)
                else:
                    act(d, o)
                store("s", T.y[:, a:b], ap(d), d)
            quant(r("vq"), r("vp"), r("vb"))
            out(1, "a")
            tt(r("M", 96, 120), slot("FD", 3), slot("base", 3), A.add)
            tsp(r("Yc"), last("SC"), scl(0), None, A.mult)
            copy(r("Pc"), r("M", 96, 120))
            gact(r("yo"), r("idw"), r("Yc"))
            gact(r("po"), r("idw"), r("Pc"))
            store("s", T.pl[:, 0:384], T.yo[0:128:16, :], r("yo"))
            store("a", T.pl[:, 384:768], T.po[0:128:16, :], r("po"))
        for b in range(4):
            o = ps("psA", b, 192)
            mm(o, r("eq", 128 * b, 128 * b + 128), r("ep", 128 * b, 128 * b + 128), r("hlq" + me), r("hlp" + me))
            d = r("X", b, 768, 4)
            tt(d, o, d, A.add)
    out(0, "v")
    g.wait_ge(T.sem.snd, sent[0])
    g.wait_ge(T.sem.stS, stores["s"])
    g.wait_ge(T.sem.stA, stores["a"])
    for q in ("g", "v", "a", "t"):
        need("g", [("q" + q, count[q])])
